import numpy as np, ml_dtypes
CORES = [120,124,248,252,376,380,504,508]
N = 8
import mx_ref
NC, KT = 128, 2
BF = ml_dtypes.bfloat16
def setup_inputs(rng):
    def f(*shape):
        return mx_ref.flush((rng.standard_normal(shape, dtype=np.float32) * np.exp2(rng.integers(-2, 3, shape[:-1] + (1,)))).astype(BF))
    return {"w": f(N, 128, KT * 512), "x": f(N, 128, KT * 4 * NC)}
def setup_inputs_blocks(rng):
    d = setup_inputs(rng)
    for k in ("w", "x"): d[k] = mx_ref.spread(d[k], rng, 4)
    return d
def setup_inputs_wide(rng):
    d = setup_inputs(rng)
    for k in ("w", "x"): d[k] = mx_ref.flush((d[k].astype(np.float32) * np.exp2(rng.integers(-8, 9, (N, 1, 1))).astype(np.float32)).astype(BF))
    return d
def setup_inputs_zeros(rng):
    d = setup_inputs(rng); v = d["x"].reshape(N, 128, -1, 4).copy()
    v[np.broadcast_to((rng.random((N, 1, v.shape[2], 1)) < 0.33), v.shape)] = 0
    d["x"] = v.reshape(d["x"].shape)
    return d
def reference(w, x):
    QW = [[mx_ref.quantize(w[r][:, 512 * t:512 * t + 512]) for t in range(KT)] for r in range(N)]
    QX = [[mx_ref.quantize(x[j][:, 4 * NC * t:4 * NC * t + 4 * NC]) for t in range(KT)] for j in range(N)]
    y = np.zeros((N, 128, N * NC), np.float32)
    for r in range(N):
        for j in range(N):
            for t in range(KT):
                p = mx_ref.matmul(QW[r][t], QX[j][t])
                y[r][:, NC * j:NC * j + NC] = p if t == 0 else y[r][:, NC * j:NC * j + NC] + p
    return {"y": y}

@@ -1,0 +1,139 @@
+from concourse.bass import DstId, RemoteDMATransfer
+from concourse.mybir import dt, ActivationFunctionType
+
+N, KT, NC = 8, 2, 128
+BW = KT * NC
+BANK = 512
+
+SCRATCH = {
+    "xin": ("sbuf", [128, 4 * BW], "bfloat16"),
+    "win": ("sbuf", [128, 4 * BW], "bfloat16"),
+    "xq": ("sbuf", [128, N * BW], "float8_e4m3fn_x4"),
+    "xs": ("sbuf", [128, N * BW], "uint8"),
+    "wq": ("sbuf", [128, BW], "float8_e4m3fn_x4"),
+    "ws": ("sbuf", [128, BW], "uint8"),
+    "acc": ("psum", [128, N * BANK], "float32"),
+    "yb": ("sbuf", [128, N * NC], "float32"),
+}
+SEMAPHORES = (["ldx", "ldw", "qx", "qw", "sent", "cpv", "cps", "st"]
+              + ["ac%d" % j for j in range(N)] + ["as%d" % j for j in range(N)] + ["mm%d" % j for j in range(N)])
+
+
+def _ones(mask):
+    return bin(mask).count("1")
+
+
+def _every_other(mask, first):
+    bits = [b for b in range(mask.bit_length()) if (mask >> b) & 1]
+    out = 0
+    for b in bits[first::2]:
+        out |= 1 << b
+    return out
+
+
+def _around(core, cores, topo):
+    peer = [o for o in cores if o != core and topo.host(o) == topo.host(core) and topo.chip(o) == topo.chip(core)][0]
+    plane = [o for o in cores if topo.same_plane(core, o)]
+    far = [o for o in cores if topo.rack(topo.host(o)) != topo.rack(topo.host(core))]
+    cable = [o for o in far if topo.may_write(core, o)]
+    diag = [o for o in far if not topo.may_write(core, o)]
+
+    def split(grp):
+        return ([o for o in grp if topo.die(o) == topo.die(core)][0], [o for o in grp if topo.die(o) != topo.die(core)][0])
+
+    return peer, split(plane), split(cable), split(diag)
+
+
+def _plan(core, cores, topo):
+    peer, (pt, po), (ct, co), _ = _around(core, cores, topo)
+    off = topo.mask(core, pt) & topo.mask(core, ct)
+    sw, cb = _every_other(off, 0), _every_other(off, 1)
+    on = topo.mask(core, peer) & ~off
+    steps = []
+    for kind in "cs":
+        steps.append((False, kind, core, [(ct, cb), (pt, sw)]))
+    for kind in "cs":
+        steps.append((False, kind, core, [(peer, on)]))
+    for kind in "cs":
+        steps.append((True, kind, ct, [(po, sw), (peer, on)]))
+        steps.append((True, kind, pt, [(ct, cb), (peer, on)]))
+    return steps
+
+
+def rank_program(g, core, T, topo):
+    rank = T.rank_of(core)
+    if rank is None:
+        return
+    cores = list(T.cores)
+    sem = T.sem
+    rk = dict((c, T.rank_of(c)) for c in cores)
+
+    def view(kind, j):
+        if kind == "c":
+            return T.xq[:, BW * j:BW * (j + 1)].bitcast(dt.uint8)
+        return T.xs[:, BW * j:BW * (j + 1)]
+
+    due = {}
+    for s in cores:
+        for _, kind, blk, outs in _plan(s, cores, topo):
+            for dst, mask in outs:
+                if dst == core:
+                    due[(kind, blk)] = due.get((kind, blk), 0) + _ones(mask)
+
+    g.sync.dma_start(out=T.xin[:], in_=T.x[:]).then_inc(sem.ldx, 16)
+    g.sync.dma_start(out=T.win[:], in_=T.w[:]).then_inc(sem.ldw, 16)
+    g.vector.wait_ge(sem.ldx, 16)
+    g.vector.quantize_mx(out=T.xq[:, BW * rank:BW * (rank + 1)], scales=T.xs[:, BW * rank:BW * (rank + 1)],
+                         in_=T.xin[:]).then_inc(sem.qx, 1)
+    g.vector.wait_ge(sem.ldw, 16)
+    g.vector.quantize_mx(out=T.wq[:], scales=T.ws[:], in_=T.win[:]).then_inc(sem.qw, 1)
+
+    g.wait_ge(sem.qx, 1)
+    sent = 0
+    for wait, kind, blk, outs in _plan(core, cores, topo):
+        j = rk[blk]
+        arrive = sem["a%s%d" % (kind, j)]
+        if wait:
+            g.wait_ge(arrive, due[(kind, blk)])
+        trs = []
+        for dst, mask in outs:
+            rid, pid = topo.addr(dst, core)
+            trs.append(RemoteDMATransfer(dst_ids=[DstId(rid=rid, pnc=pid)], dma_engine_mask=mask, remote_sem=arrive,
+                                         src=view(kind, j), dst=view(kind, j)))
+            sent += _ones(mask)
+        g.remote_dma_fused(trs, local_sem=sem.sent)
+
+    peer, (pt, po), (ct, co), (dg, do) = _around(core, cores, topo)
+    order = [core, peer, ct, pt, co, po, do, dg]
+    g.tensor.wait_ge(sem.qw, 1)
+    g.tensor.wait_ge(sem.qx, 1)
+    for blk in order:
+        j = rk[blk]
+        if blk != core:
+            g.tensor.wait_ge(sem["ac%d" % j], due[("c", blk)])
+            g.tensor.wait_ge(sem["as%d" % j], due[("s", blk)])
+        for t in range(KT):
+            a, b = BW * j + NC * t, BW * j + NC * (t + 1)
+            g.tensor.matmul_mx(out=T.acc[:, BANK * j:BANK * j + NC],
+                               lhsT=T.wq[:, NC * t:NC * (t + 1)], lhsT_scale=T.ws[:, NC * t:NC * (t + 1)],
+                               rhs=T.xq[:, a:b], rhs_scale=T.xs[:, a:b],
+                               start=(t == 0), stop=(t == KT - 1)).then_inc(sem["mm%d" % j], 1)
+
+    nv = ns = 0
+    for i, blk in enumerate(order):
+        j = rk[blk]
+        out, in_ = T.yb[:, NC * j:NC * (j + 1)], T.acc[:, BANK * j:BANK * j + NC]
+        if i % 2 == 0:
+            g.vector.wait_ge(sem["mm%d" % j], KT)
+            g.vector.tensor_copy(out=out, in_=in_).then_inc(sem.cpv, 1)
+            nv += 1
+        else:
+            g.scalar.wait_ge(sem["mm%d" % j], KT)
+            g.scalar.activation(out=out, in_=in_, func=ActivationFunctionType.Copy).then_inc(sem.cps, 1)
+            ns += 1
+
+    g.sync.wait_ge(sem.cpv, nv)
+    g.sync.wait_ge(sem.cps, ns)
+    g.sync.dma_start(out=T.y[:], in_=T.yb[:]).then_inc(sem.st, 16)
+    g.sync.wait_ge(sem.st, 16)
+    g.wait_ge(sem.sent, sent)

@@ -4,6 +4,8 @@ from concourse.mybir import dt, ActivationFunctionType
 N, KT, NC = 8, 2, 128
 BW = KT * NC
 BANK = 512
+PIECE = {"c": (True, 0, BW, KT), "e": (True, 0, NC, 1), "f": (True, NC, BW, KT), "s": (False, 0, BW, KT)}
+READS = (("e", "s"), ("f",))
 
 SCRATCH = {
     "xin": ("sbuf", [128, 4 * BW], "bfloat16"),
@@ -15,8 +17,9 @@ SCRATCH = {
     "acc": ("psum", [128, N * BANK], "float32"),
     "yb": ("sbuf", [128, N * NC], "float32"),
 }
-SEMAPHORES = (["ldx", "ldw", "qx", "qw", "sent", "cpv", "cps", "st"]
-              + ["ac%d" % j for j in range(N)] + ["as%d" % j for j in range(N)] + ["mm%d" % j for j in range(N)])
+SEMAPHORES = (["ldw", "qw", "sent", "st", "st2"] + ["ldx%d" % t for t in range(KT)] + ["qx%d" % t for t in range(KT)]
+              + ["a%s%d" % (k, j) for k in sorted(PIECE) for j in range(N)]
+              + ["mm%d" % j for j in range(N)] + ["cp%d" % j for j in range(N)])
 
 
 def _ones(mask):
@@ -50,14 +53,24 @@ def _plan(core, cores, topo):
     sw, cb = _every_other(off, 0), _every_other(off, 1)
     on = topo.mask(core, peer) & ~off
     steps = []
-    for kind in "cs":
-        steps.append((False, kind, core, [(ct, cb), (pt, sw)]))
-    for kind in "cs":
-        steps.append((False, kind, core, [(peer, on)]))
-    for kind in "cs":
-        steps.append((True, kind, ct, [(po, sw), (peer, on)]))
-        steps.append((True, kind, pt, [(ct, cb), (peer, on)]))
+    for k in "esf":
+        steps.append([(k, core, ct, cb), (k, core, pt, sw)])
+    for k in "cs":
+        steps.append([(k, core, peer, on)])
+    for k in "esf":
+        steps.append([(k, ct, po, sw), (k, ct, peer, on)])
+        steps.append([(k, pt, ct, cb), (k, pt, peer, on)])
     return steps
+
+
+def _runs(js):
+    out = []
+    for j in sorted(js):
+        if out and out[-1][1] == j:
+            out[-1][1] = j + 1
+        else:
+            out.append([j, j + 1])
+    return out
 
 
 def rank_program(g, core, T, topo):
@@ -68,72 +81,83 @@ def rank_program(g, core, T, topo):
     sem = T.sem
     rk = dict((c, T.rank_of(c)) for c in cores)
 
-    def view(kind, j):
-        if kind == "c":
-            return T.xq[:, BW * j:BW * (j + 1)].bitcast(dt.uint8)
-        return T.xs[:, BW * j:BW * (j + 1)]
+    def view(k, j):
+        a, b = BW * j + PIECE[k][1], BW * j + PIECE[k][2]
+        if PIECE[k][0]:
+            return T.xq[:, a:b].bitcast(dt.uint8)
+        return T.xs[:, a:b]
 
     due = {}
     for s in cores:
-        for _, kind, blk, outs in _plan(s, cores, topo):
-            for dst, mask in outs:
+        for writes in _plan(s, cores, topo):
+            for k, blk, dst, mask in writes:
                 if dst == core:
-                    due[(kind, blk)] = due.get((kind, blk), 0) + _ones(mask)
+                    due[(k, blk)] = due.get((k, blk), 0) + _ones(mask)
 
-    g.sync.dma_start(out=T.xin[:], in_=T.x[:]).then_inc(sem.ldx, 16)
+    for t in range(KT):
+        g.sync.dma_start(out=T.xin[:, 4 * NC * t:4 * NC * (t + 1)],
+                         in_=T.x[:, 4 * NC * t:4 * NC * (t + 1)]).then_inc(sem["ldx%d" % t], 16)
     g.sync.dma_start(out=T.win[:], in_=T.w[:]).then_inc(sem.ldw, 16)
-    g.vector.wait_ge(sem.ldx, 16)
-    g.vector.quantize_mx(out=T.xq[:, BW * rank:BW * (rank + 1)], scales=T.xs[:, BW * rank:BW * (rank + 1)],
-                         in_=T.xin[:]).then_inc(sem.qx, 1)
+    for t in range(KT):
+        a, b = BW * rank + NC * t, BW * rank + NC * (t + 1)
+        g.vector.wait_ge(sem["ldx%d" % t], 16)
+        g.vector.quantize_mx(out=T.xq[:, a:b], scales=T.xs[:, a:b],
+                             in_=T.xin[:, 4 * NC * t:4 * NC * (t + 1)]).then_inc(sem["qx%d" % t], 1)
     g.vector.wait_ge(sem.ldw, 16)
     g.vector.quantize_mx(out=T.wq[:], scales=T.ws[:], in_=T.win[:]).then_inc(sem.qw, 1)
 
-    g.wait_ge(sem.qx, 1)
-    sent = 0
-    for wait, kind, blk, outs in _plan(core, cores, topo):
+    sent = packed = 0
+    for writes in _plan(core, cores, topo):
+        k, blk = writes[0][0], writes[0][1]
         j = rk[blk]
-        arrive = sem["a%s%d" % (kind, j)]
-        if wait:
-            g.wait_ge(arrive, due[(kind, blk)])
+        arrive = sem["a%s%d" % (k, j)]
+        if blk == core:
+            while packed < PIECE[k][3]:
+                g.wait_ge(sem["qx%d" % packed], 1)
+                packed += 1
+        else:
+            g.wait_ge(arrive, due[(k, blk)])
         trs = []
-        for dst, mask in outs:
+        for _, _, dst, mask in writes:
             rid, pid = topo.addr(dst, core)
             trs.append(RemoteDMATransfer(dst_ids=[DstId(rid=rid, pnc=pid)], dma_engine_mask=mask, remote_sem=arrive,
-                                         src=view(kind, j), dst=view(kind, j)))
+                                         src=view(k, j), dst=view(k, j)))
             sent += _ones(mask)
         g.remote_dma_fused(trs, local_sem=sem.sent)
 
     peer, (pt, po), (ct, co), (dg, do) = _around(core, cores, topo)
-    order = [core, peer, ct, pt, co, po, do, dg]
+    first, last = [core, peer, ct, pt], [co, po, do, dg]
+    jobs = [(blk, t) for blk in first for t in range(KT)] + [(blk, t) for t in range(KT) for blk in last]
     g.tensor.wait_ge(sem.qw, 1)
-    g.tensor.wait_ge(sem.qx, 1)
-    for blk in order:
+    for t in range(KT):
+        g.tensor.wait_ge(sem["qx%d" % t], 1)
+    for blk, t in jobs:
         j = rk[blk]
-        if blk != core:
-            g.tensor.wait_ge(sem["ac%d" % j], due[("c", blk)])
-            g.tensor.wait_ge(sem["as%d" % j], due[("s", blk)])
-        for t in range(KT):
-            a, b = BW * j + NC * t, BW * j + NC * (t + 1)
-            g.tensor.matmul_mx(out=T.acc[:, BANK * j:BANK * j + NC],
-                               lhsT=T.wq[:, NC * t:NC * (t + 1)], lhsT_scale=T.ws[:, NC * t:NC * (t + 1)],
-                               rhs=T.xq[:, a:b], rhs_scale=T.xs[:, a:b],
-                               start=(t == 0), stop=(t == KT - 1)).then_inc(sem["mm%d" % j], 1)
+        for k in (READS[t] if ("e", blk) in due else "cs" if t == 0 else ""):
+            if (k, blk) in due:
+                g.tensor.wait_ge(sem["a%s%d" % (k, j)], due[(k, blk)])
+        a, b = BW * j + NC * t, BW * j + NC * (t + 1)
+        g.tensor.matmul_mx(out=T.acc[:, BANK * j:BANK * j + NC],
+                           lhsT=T.wq[:, NC * t:NC * (t + 1)], lhsT_scale=T.ws[:, NC * t:NC * (t + 1)],
+                           rhs=T.xq[:, a:b], rhs_scale=T.xs[:, a:b],
+                           start=(t == 0), stop=(t == KT - 1)).then_inc(sem["mm%d" % j], 1)
 
-    nv = ns = 0
-    for i, blk in enumerate(order):
+    for i, blk in enumerate(first + last):
         j = rk[blk]
         out, in_ = T.yb[:, NC * j:NC * (j + 1)], T.acc[:, BANK * j:BANK * j + NC]
         if i % 2 == 0:
             g.vector.wait_ge(sem["mm%d" % j], KT)
-            g.vector.tensor_copy(out=out, in_=in_).then_inc(sem.cpv, 1)
-            nv += 1
+            g.vector.tensor_copy(out=out, in_=in_).then_inc(sem["cp%d" % j], 1)
         else:
             g.scalar.wait_ge(sem["mm%d" % j], KT)
-            g.scalar.activation(out=out, in_=in_, func=ActivationFunctionType.Copy).then_inc(sem.cps, 1)
-            ns += 1
+            g.scalar.activation(out=out, in_=in_, func=ActivationFunctionType.Copy).then_inc(sem["cp%d" % j], 1)
 
-    g.sync.wait_ge(sem.cpv, nv)
-    g.sync.wait_ge(sem.cps, ns)
-    g.sync.dma_start(out=T.y[:], in_=T.yb[:]).then_inc(sem.st, 16)
-    g.sync.wait_ge(sem.st, 16)
+    for q, grp, done in ((g.sync, [core, peer, ct, pt, co, po], sem.st), (g.scalar, [do, dg], sem.st2)):
+        for blk in grp:
+            q.wait_ge(sem["cp%d" % rk[blk]], 1)
+        n = 0
+        for a, b in _runs([rk[blk] for blk in grp]):
+            q.dma_start(out=T.y[:, NC * a:NC * b], in_=T.yb[:, NC * a:NC * b]).then_inc(done, 16)
+            n += 16
+        q.wait_ge(done, n)
     g.wait_ge(sem.sent, sent)

@@ -17,7 +17,7 @@ SCRATCH = {
     "acc": ("psum", [128, N * BANK], "float32"),
     "yb": ("sbuf", [128, N * NC], "float32"),
 }
-SEMAPHORES = (["ldw", "qw", "sent", "st", "st2"] + ["ldx%d" % t for t in range(KT)] + ["qx%d" % t for t in range(KT)]
+SEMAPHORES = (["ldw", "qw", "sent", "st0", "st1", "st2"] + ["ldx%d" % t for t in range(KT)] + ["qx%d" % t for t in range(KT)]
               + ["a%s%d" % (k, j) for k in sorted(PIECE) for j in range(N)]
               + ["mm%d" % j for j in range(N)] + ["cp%d" % j for j in range(N)])
 
@@ -47,19 +47,38 @@ def _around(core, cores, topo):
     return peer, split(plane), split(cable), split(diag)
 
 
+def _spares(q, cores, topo):
+    n = topo.CORES_PER_CHIP
+    near = [c for c in range(max(q - n, 0), q + n + 1)
+            if c not in cores and topo.host(c) == topo.host(q) and topo.chip(c) == topo.chip(q) and topo.die(c) == topo.die(q)]
+    near.sort(key=lambda c: abs(c - q))
+    return near[-1], near[-2]
+
+
 def _plan(core, cores, topo):
-    peer, (pt, po), (ct, co), _ = _around(core, cores, topo)
-    off = topo.mask(core, pt) & topo.mask(core, ct)
-    sw, cb = _every_other(off, 0), _every_other(off, 1)
-    on = topo.mask(core, peer) & ~off
     steps = []
-    for k in "esf":
-        steps.append([(k, core, ct, cb), (k, core, pt, sw)])
-    for k in "cs":
-        steps.append([(k, core, peer, on)])
-    for k in "esf":
-        steps.append([(k, ct, po, sw), (k, ct, peer, on)])
-        steps.append([(k, pt, ct, cb), (k, pt, peer, on)])
+    if core in cores:
+        peer, (pt, po), (ct, co), _ = _around(core, cores, topo)
+        by_sw, by_cb = _spares(pt, cores, topo)[0], _spares(ct, cores, topo)[1]
+        off = topo.mask(core, by_sw) & topo.mask(core, by_cb)
+        sw, cb = _every_other(off, 0), _every_other(off, 1)
+        on = topo.mask(core, peer) & ~off
+        for k in "esf":
+            steps.append([(k, core, by_cb, cb), (k, core, by_sw, sw)])
+        for k in "cs":
+            steps.append([(k, core, peer, on)])
+        return steps
+    for q in cores:
+        role = _spares(q, cores, topo)
+        if core not in role:
+            continue
+        peer, (pt, po), (ct, co), _ = _around(q, cores, topo)
+        blk, far = (pt, ct) if core == role[0] else (ct, po)
+        off = topo.mask(core, far)
+        on = topo.mask(core, q) & topo.mask(core, peer) & ~off
+        for k in "esf":
+            steps.append([(k, blk, far, _every_other(off, 0)), (k, blk, q, _every_other(on, 1)),
+                          (k, blk, peer, _every_other(on, 0))])
     return steps
 
 
@@ -74,10 +93,11 @@ def _runs(js):
 
 
 def rank_program(g, core, T, topo):
-    rank = T.rank_of(core)
-    if rank is None:
-        return
     cores = list(T.cores)
+    rank = T.rank_of(core)
+    spares = [c for q in cores for c in _spares(q, cores, topo)]
+    if rank is None and core not in spares:
+        return
     sem = T.sem
     rk = dict((c, T.rank_of(c)) for c in cores)
 
@@ -88,23 +108,24 @@ def rank_program(g, core, T, topo):
         return T.xs[:, a:b]
 
     due = {}
-    for s in cores:
+    for s in cores + spares:
         for writes in _plan(s, cores, topo):
             for k, blk, dst, mask in writes:
                 if dst == core:
                     due[(k, blk)] = due.get((k, blk), 0) + _ones(mask)
 
-    for t in range(KT):
-        g.sync.dma_start(out=T.xin[:, 4 * NC * t:4 * NC * (t + 1)],
-                         in_=T.x[:, 4 * NC * t:4 * NC * (t + 1)]).then_inc(sem["ldx%d" % t], 16)
-    g.sync.dma_start(out=T.win[:], in_=T.w[:]).then_inc(sem.ldw, 16)
-    for t in range(KT):
-        a, b = BW * rank + NC * t, BW * rank + NC * (t + 1)
-        g.vector.wait_ge(sem["ldx%d" % t], 16)
-        g.vector.quantize_mx(out=T.xq[:, a:b], scales=T.xs[:, a:b],
-                             in_=T.xin[:, 4 * NC * t:4 * NC * (t + 1)]).then_inc(sem["qx%d" % t], 1)
-    g.vector.wait_ge(sem.ldw, 16)
-    g.vector.quantize_mx(out=T.wq[:], scales=T.ws[:], in_=T.win[:]).then_inc(sem.qw, 1)
+    if rank is not None:
+        for t in range(KT):
+            g.sync.dma_start(out=T.xin[:, 4 * NC * t:4 * NC * (t + 1)],
+                             in_=T.x[:, 4 * NC * t:4 * NC * (t + 1)]).then_inc(sem["ldx%d" % t], 16)
+        g.sync.dma_start(out=T.win[:], in_=T.w[:]).then_inc(sem.ldw, 16)
+        for t in range(KT):
+            a, b = BW * rank + NC * t, BW * rank + NC * (t + 1)
+            g.vector.wait_ge(sem["ldx%d" % t], 16)
+            g.vector.quantize_mx(out=T.xq[:, a:b], scales=T.xs[:, a:b],
+                                 in_=T.xin[:, 4 * NC * t:4 * NC * (t + 1)]).then_inc(sem["qx%d" % t], 1)
+        g.vector.wait_ge(sem.ldw, 16)
+        g.vector.quantize_mx(out=T.wq[:], scales=T.ws[:], in_=T.win[:]).then_inc(sem.qw, 1)
 
     sent = packed = 0
     for writes in _plan(core, cores, topo):
@@ -124,9 +145,12 @@ def rank_program(g, core, T, topo):
                                          src=view(k, j), dst=view(k, j)))
             sent += _ones(mask)
         g.remote_dma_fused(trs, local_sem=sem.sent)
+    if rank is None:
+        g.wait_ge(sem.sent, sent)
+        return
 
     peer, (pt, po), (ct, co), (dg, do) = _around(core, cores, topo)
-    first, last = [core, peer, ct, pt], [co, po, do, dg]
+    first, last = [core, peer], [ct, pt, co, po, do, dg]
     jobs = [(blk, t) for blk in first for t in range(KT)] + [(blk, t) for t in range(KT) for blk in last]
     g.tensor.wait_ge(sem.qw, 1)
     for t in range(KT):
@@ -152,12 +176,15 @@ def rank_program(g, core, T, topo):
             g.scalar.wait_ge(sem["mm%d" % j], KT)
             g.scalar.activation(out=out, in_=in_, func=ActivationFunctionType.Copy).then_inc(sem["cp%d" % j], 1)
 
-    for q, grp, done in ((g.sync, [core, peer, ct, pt, co, po], sem.st), (g.scalar, [do, dg], sem.st2)):
+    waits = []
+    for q, grp, done in ((g.sync, [core, peer], sem.st0), (g.sync, [ct, pt, co, po], sem.st1), (g.scalar, [do, dg], sem.st2)):
         for blk in grp:
             q.wait_ge(sem["cp%d" % rk[blk]], 1)
         n = 0
         for a, b in _runs([rk[blk] for blk in grp]):
             q.dma_start(out=T.y[:, NC * a:NC * b], in_=T.yb[:, NC * a:NC * b]).then_inc(done, 16)
             n += 16
+        waits.append((q, done, n))
+    for q, done, n in waits:
         q.wait_ge(done, n)
     g.wait_ge(sem.sent, sent)

from concourse.bass import DstId, RemoteDMATransfer
from concourse.mybir import dt, ActivationFunctionType

N, KT, NC = 8, 2, 128
BW = KT * NC
BANK = 512
PIECE = {"c": (True, 0, BW, KT), "e": (True, 0, NC, 1), "f": (True, NC, BW, KT), "s": (False, 0, BW, KT)}
READS = (("e", "s"), ("f",))

SCRATCH = {
    "xin": ("sbuf", [128, 4 * BW], "bfloat16"),
    "win": ("sbuf", [128, 4 * BW], "bfloat16"),
    "xq": ("sbuf", [128, N * BW], "float8_e4m3fn_x4"),
    "xs": ("sbuf", [128, N * BW], "uint8"),
    "wq": ("sbuf", [128, BW], "float8_e4m3fn_x4"),
    "ws": ("sbuf", [128, BW], "uint8"),
    "acc": ("psum", [128, N * BANK], "float32"),
    "yb": ("sbuf", [128, N * NC], "float32"),
}
SEMAPHORES = (["ldw", "qw", "sent", "st0", "st1", "st2"] + ["ldx%d" % t for t in range(KT)] + ["qx%d" % t for t in range(KT)]
              + ["a%s%d" % (k, j) for k in sorted(PIECE) for j in range(N)]
              + ["mm%d" % j for j in range(N)] + ["cp%d" % j for j in range(N)])


def _ones(mask):
    return bin(mask).count("1")


def _every_other(mask, first):
    bits = [b for b in range(mask.bit_length()) if (mask >> b) & 1]
    out = 0
    for b in bits[first::2]:
        out |= 1 << b
    return out


def _around(core, cores, topo):
    peer = [o for o in cores if o != core and topo.host(o) == topo.host(core) and topo.chip(o) == topo.chip(core)][0]
    plane = [o for o in cores if topo.same_plane(core, o)]
    far = [o for o in cores if topo.rack(topo.host(o)) != topo.rack(topo.host(core))]
    cable = [o for o in far if topo.may_write(core, o)]
    diag = [o for o in far if not topo.may_write(core, o)]

    def split(grp):
        return ([o for o in grp if topo.die(o) == topo.die(core)][0], [o for o in grp if topo.die(o) != topo.die(core)][0])

    return peer, split(plane), split(cable), split(diag)


def _spares(q, cores, topo):
    n = topo.CORES_PER_CHIP
    near = [c for c in range(max(q - n, 0), q + n + 1)
            if c not in cores and topo.host(c) == topo.host(q) and topo.chip(c) == topo.chip(q) and topo.die(c) == topo.die(q)]
    near.sort(key=lambda c: abs(c - q))
    return near[-1], near[-2]


def _plan(core, cores, topo):
    steps = []
    if core in cores:
        peer, (pt, po), (ct, co), _ = _around(core, cores, topo)
        by_sw, by_cb = _spares(pt, cores, topo)[0], _spares(ct, cores, topo)[1]
        off = topo.mask(core, by_sw) & topo.mask(core, by_cb)
        sw, cb = _every_other(off, 0), _every_other(off, 1)
        on = topo.mask(core, peer) & ~off
        for k in "esf":
            steps.append([(k, core, by_cb, cb), (k, core, by_sw, sw)])
        for k in "cs":
            steps.append([(k, core, peer, on)])
        return steps
    for q in cores:
        role = _spares(q, cores, topo)
        if core not in role:
            continue
        peer, (pt, po), (ct, co), _ = _around(q, cores, topo)
        blk, far = (pt, ct) if core == role[0] else (ct, po)
        off = topo.mask(core, far)
        on = topo.mask(core, q) & topo.mask(core, peer) & ~off
        for k in "esf":
            steps.append([(k, blk, far, _every_other(off, 0)), (k, blk, q, _every_other(on, 1)),
                          (k, blk, peer, _every_other(on, 0))])
    return steps


def _runs(js):
    out = []
    for j in sorted(js):
        if out and out[-1][1] == j:
            out[-1][1] = j + 1
        else:
            out.append([j, j + 1])
    return out


def rank_program(g, core, T, topo):
    cores = list(T.cores)
    rank = T.rank_of(core)
    spares = [c for q in cores for c in _spares(q, cores, topo)]
    if rank is None and core not in spares:
        return
    sem = T.sem
    rk = dict((c, T.rank_of(c)) for c in cores)

    def view(k, j):
        a, b = BW * j + PIECE[k][1], BW * j + PIECE[k][2]
        if PIECE[k][0]:
            return T.xq[:, a:b].bitcast(dt.uint8)
        return T.xs[:, a:b]

    due = {}
    for s in cores + spares:
        for writes in _plan(s, cores, topo):
            for k, blk, dst, mask in writes:
                if dst == core:
                    due[(k, blk)] = due.get((k, blk), 0) + _ones(mask)

    if rank is not None:
        for t in range(KT):
            g.sync.dma_start(out=T.xin[:, 4 * NC * t:4 * NC * (t + 1)],
                             in_=T.x[:, 4 * NC * t:4 * NC * (t + 1)]).then_inc(sem["ldx%d" % t], 16)
        g.sync.dma_start(out=T.win[:], in_=T.w[:]).then_inc(sem.ldw, 16)
        for t in range(KT):
            a, b = BW * rank + NC * t, BW * rank + NC * (t + 1)
            g.vector.wait_ge(sem["ldx%d" % t], 16)
            g.vector.quantize_mx(out=T.xq[:, a:b], scales=T.xs[:, a:b],
                                 in_=T.xin[:, 4 * NC * t:4 * NC * (t + 1)]).then_inc(sem["qx%d" % t], 1)
        g.vector.wait_ge(sem.ldw, 16)
        g.vector.quantize_mx(out=T.wq[:], scales=T.ws[:], in_=T.win[:]).then_inc(sem.qw, 1)

    sent = packed = 0
    for writes in _plan(core, cores, topo):
        k, blk = writes[0][0], writes[0][1]
        j = rk[blk]
        arrive = sem["a%s%d" % (k, j)]
        if blk == core:
            while packed < PIECE[k][3]:
                g.wait_ge(sem["qx%d" % packed], 1)
                packed += 1
        else:
            g.wait_ge(arrive, due[(k, blk)])
        trs = []
        for _, _, dst, mask in writes:
            rid, pid = topo.addr(dst, core)
            trs.append(RemoteDMATransfer(dst_ids=[DstId(rid=rid, pnc=pid)], dma_engine_mask=mask, remote_sem=arrive,
                                         src=view(k, j), dst=view(k, j)))
            sent += _ones(mask)
        g.remote_dma_fused(trs, local_sem=sem.sent)
    if rank is None:
        g.wait_ge(sem.sent, sent)
        return

    peer, (pt, po), (ct, co), (dg, do) = _around(core, cores, topo)
    first, last = [core, peer], [ct, pt, co, po, do, dg]
    jobs = [(blk, t) for blk in first for t in range(KT)] + [(blk, t) for t in range(KT) for blk in last]
    g.tensor.wait_ge(sem.qw, 1)
    for t in range(KT):
        g.tensor.wait_ge(sem["qx%d" % t], 1)
    for blk, t in jobs:
        j = rk[blk]
        for k in (READS[t] if ("e", blk) in due else "cs" if t == 0 else ""):
            if (k, blk) in due:
                g.tensor.wait_ge(sem["a%s%d" % (k, j)], due[(k, blk)])
        a, b = BW * j + NC * t, BW * j + NC * (t + 1)
        g.tensor.matmul_mx(out=T.acc[:, BANK * j:BANK * j + NC],
                           lhsT=T.wq[:, NC * t:NC * (t + 1)], lhsT_scale=T.ws[:, NC * t:NC * (t + 1)],
                           rhs=T.xq[:, a:b], rhs_scale=T.xs[:, a:b],
                           start=(t == 0), stop=(t == KT - 1)).then_inc(sem["mm%d" % j], 1)

    for i, blk in enumerate(first + last):
        j = rk[blk]
        out, in_ = T.yb[:, NC * j:NC * (j + 1)], T.acc[:, BANK * j:BANK * j + NC]
        if i % 2 == 0:
            g.vector.wait_ge(sem["mm%d" % j], KT)
            g.vector.tensor_copy(out=out, in_=in_).then_inc(sem["cp%d" % j], 1)
        else:
            g.scalar.wait_ge(sem["mm%d" % j], KT)
            g.scalar.activation(out=out, in_=in_, func=ActivationFunctionType.Copy).then_inc(sem["cp%d" % j], 1)

    waits = []
    for q, grp, done in ((g.sync, [core, peer], sem.st0), (g.sync, [ct, pt, co, po], sem.st1), (g.scalar, [do, dg], sem.st2)):
        for blk in grp:
            q.wait_ge(sem["cp%d" % rk[blk]], 1)
        n = 0
        for a, b in _runs([rk[blk] for blk in grp]):
            q.dma_start(out=T.y[:, NC * a:NC * b], in_=T.yb[:, NC * a:NC * b]).then_inc(done, 16)
            n += 16
        waits.append((q, done, n))
    for q, done, n in waits:
        q.wait_ge(done, n)
    g.wait_ge(sem.sent, sent)
